import numpy as np, ml_dtypes
CORES = [24,26,29,31,48,50,53,55]
N = 8
import mx_ref
NC, WT = 512, 1
BF = ml_dtypes.bfloat16
def setup_inputs(rng):
    def f(*shape):
        return mx_ref.flush((rng.standard_normal(shape, dtype=np.float32) * np.exp2(rng.integers(-2, 3, shape[:-1] + (1,)))).astype(BF))
    return {"w": f(N, 128, WT * 512), "x": f(N, 128, 4 * NC)}
def setup_inputs_blocks(rng):
    d = setup_inputs(rng)
    for k in ("w", "x"): d[k] = mx_ref.spread(d[k], rng, 4)
    return d
def setup_inputs_wide(rng):
    d = setup_inputs(rng)
    for k in ("w", "x"): d[k] = mx_ref.flush((d[k].astype(np.float32) * np.exp2(rng.integers(-8, 9, (N, 1, 1))).astype(np.float32)).astype(BF))
    return d
def setup_inputs_zeros(rng):
    d = setup_inputs(rng); v = d["x"].reshape(N, 128, -1, 4).copy()
    v[np.broadcast_to((rng.random((N, 1, v.shape[2], 1)) < 0.33), v.shape)] = 0
    d["x"] = v.reshape(d["x"].shape)
    return d
def reference(w, x):
    QW = [mx_ref.quantize(w[b // WT][:, 512 * (b % WT):512 * (b % WT) + 512]) for b in range(N * WT)]
    y = np.zeros((N, 128, N * WT * NC), np.float32)
    for r in range(N):
        qx = mx_ref.quantize(x[r])
        for b in range(N * WT):
            y[r][:, NC * b:NC * b + NC] = mx_ref.matmul(QW[b], qx)
    return {"y": y}

from concourse.bass import DstId, RemoteDMATransfer
from concourse.mybir import dt

N = 8
WC = 128
NC = 512

SCRATCH = {
    "wb": ("sbuf", [128, 4 * WC], "bfloat16"),
    "xb": ("sbuf", [128, 4 * NC], "bfloat16"),
    "wq": ("sbuf", [128, N * WC], "float8_e4m3fn_x4"),
    "ws": ("sbuf", [128, N * WC], "uint8"),
    "xq": ("sbuf", [128, NC], "float8_e4m3fn_x4"),
    "xs": ("sbuf", [128, NC], "uint8"),
    "ps": ("psum", [128, N * NC], "float32"),
    "yb": ("sbuf", [128, N * NC], "float32"),
}
SEMAPHORES = (["wl", "xl", "wq", "xq", "loc", "sta", "stb"]
              + ["ac%d" % j for j in range(N)] + ["as%d" % j for j in range(N)]
              + ["mm%d" % j for j in range(N)] + ["cp%d" % j for j in range(N)])


def _bits(m):
    return [e for e in range(m.bit_length()) if (m >> e) & 1]


def _mask(engines):
    m = 0
    for e in engines:
        m |= 1 << e
    return m


def _plan(T, topo):
    cores = list(T.cores)
    steps = {c: [] for c in cores}
    arrive = {c: {} for c in cores}

    def send(src, j, groups):
        steps[src].append((j, [(d, e) for d, e, _ in groups]))
        for dests, engines, key in groups:
            for k, d in enumerate(dests):
                arrive[d][j] = (len(engines), key + k)

    def near(c, cands):
        same = [p for p in cands if topo.die(p) == topo.die(c)]
        return (same or cands)[0]

    side = {}
    for a in sorted(set(topo.chip(c) for c in cores)):
        here = [c for c in cores if topo.chip(c) == a]
        there = [c for c in cores if topo.chip(c) != a]
        ports = [c for c in here if all(topo.may_write(c, d) for d in there)]
        side[a] = (here, there, ports, [c for c in here if c not in ports])

    for a, (here, there, ports, plain) in side.items():
        far_plain = side[topo.chip(there[0])][3]
        for p in plain:
            r = near(p, ports)
            on = _bits(topo.mask(p, r))
            h = len(on) // 2
            send(p, T.rank_of(p), [([r], on[:h], 10), ([c for c in here if c not in (p, r)], on[h:], 10)])
        for q in ports:
            tgt = near(q, far_plain)
            peers = [c for c in here if c != q]
            off = _bits(topo.mask(q, tgt))
            on = [e for e in _bits(topo.mask(q, peers[0])) if e not in off]
            send(q, T.rank_of(q), [([tgt], off, 20), (peers, on, 10)])
    for a, (here, there, ports, plain) in side.items():
        far_plain = side[topo.chip(there[0])][3]
        for i, q in enumerate(ports):
            turn = i * len(there) // len(ports)
            dests = there[turn:] + there[:turn]
            for p in plain:
                if near(p, ports) == q:
                    send(q, T.rank_of(p), [(dests, _bits(topo.mask(q, dests[0])), 40)])
            tgt = near(q, far_plain)
            peers = [c for c in there if c != tgt]
            send(tgt, T.rank_of(q), [(peers, _bits(topo.mask(tgt, peers[0])), 30)])
    return steps, arrive


def rank_program(g, core, T, topo):
    rank = T.rank_of(core)
    if rank is None:
        return
    steps, arrive = _plan(T, topo)
    sem = T.sem

    def codes(j):
        return T.wq[:, j * WC:(j + 1) * WC]

    def plane(j):
        return T.ws[:, j * WC:(j + 1) * WC]

    g.sync.dma_start(out=T.wb[:], in_=T.w[:]).then_inc(sem.wl, 16)
    g.sync.dma_start(out=T.xb[:], in_=T.x[:]).then_inc(sem.xl, 16)
    g.vector.wait_ge(sem.wl, 16)
    g.vector.quantize_mx(out=codes(rank), scales=plane(rank), in_=T.wb[:]).then_inc(sem.wq, 1)
    g.vector.wait_ge(sem.xl, 16)
    g.vector.quantize_mx(out=T.xq[:], scales=T.xs[:], in_=T.xb[:]).then_inc(sem.xq, 1)

    g.wait_ge(sem.wq, 1)
    left = 0
    for j, groups in steps[core]:
        for kind in ("ac", "as"):
            if j != rank:
                g.wait_ge(sem["%s%d" % (kind, j)], arrive[core][j][0])
            ap = codes(j).bitcast(dt.uint8) if kind == "ac" else plane(j)
            transfers = []
            for dests, engines in groups:
                ids = []
                for d in dests:
                    rid, pid, _ = topo.addr(d)
                    ids.append(DstId(rid=rid, pnc=pid))
                transfers.append(RemoteDMATransfer(dst_ids=ids, dma_engine_mask=_mask(engines),
                                                   remote_sem=sem["%s%d" % (kind, j)],
                                                   srcs=[ap], dsts=[ap for _ in dests]))
                left += len(engines)
            g.remote_dma_fused(transfers, local_sem=sem.loc)
    g.wait_ge(sem.loc, left)

    order = [rank] + sorted(arrive[core], key=lambda j: (arrive[core][j][1], j))
    g.tensor.wait_ge(sem.wq, 1)
    g.tensor.wait_ge(sem.xq, 1)
    stored = [0, 0]
    for k, j in enumerate(order):
        blk = slice(j * NC, (j + 1) * NC)
        if j != rank:
            g.tensor.wait_ge(sem["ac%d" % j], arrive[core][j][0])
            g.tensor.wait_ge(sem["as%d" % j], arrive[core][j][0])
        g.tensor.matmul_mx(T.ps[:, blk], codes(j), plane(j), T.xq[:], T.xs[:], True, True).then_inc(sem["mm%d" % j], 1)
        g.vector.wait_ge(sem["mm%d" % j], 1)
        g.vector.tensor_copy(out=T.yb[:, blk], in_=T.ps[:, blk]).then_inc(sem["cp%d" % j], 1)
        q, s = ((g.sync, sem.sta), (g.scalar, sem.stb))[k % 2]
        q.wait_ge(sem["cp%d" % j], 1)
        q.dma_start(out=T.y[:, blk], in_=T.yb[:, blk]).then_inc(s, 16)
        stored[k % 2] += 16
    g.sync.wait_ge(sem.sta, stored[0])
    g.scalar.wait_ge(sem.stb, stored[1])
